import numpy as np
import ml_dtypes


def mxq(x, axis, fmt="e4m3"):
    dtype, down = {"e4m3": (ml_dtypes.float8_e4m3fn, 7), "e5m2": (ml_dtypes.float8_e5m2, 14)}[fmt]
    v = np.moveaxis(np.asarray(x, np.float32).astype(ml_dtypes.bfloat16).astype(np.float64), axis, -1)
    blocks = v.reshape(v.shape[:-1] + (-1, 32))
    amax = np.abs(blocks).max(-1, keepdims=True)
    byte = np.maximum(np.where(amax > 0, np.frexp(amax)[1] - 1 + 127, 0) - down, 1)
    scale = np.exp2(byte - 127.0)
    codes = (blocks / scale).astype(np.float32).astype(dtype).astype(np.float64)
    return np.moveaxis((codes * scale).reshape(v.shape), -1, axis)


WIDE = False


def mx_kscale(k):
    if not WIDE:
        return np.ones(k)
    levels = np.array([10, -10, 5, -5, 0])
    if k % 512:
        return np.exp2(np.random.permutation(np.resize(levels, k // 32))).repeat(32)
    a = np.empty((k // 512, 16))
    for p in range(k // 512):
        a[p, :8] = np.random.permutation(np.resize(levels, 8))
        for g in range(8):
            far = levels[np.abs(levels - a[p, g]) >= 10]
            a[p, g + 8] = far[np.random.randint(len(far))]
    return np.exp2(a.ravel()).repeat(32)


def f64(x):
    return np.asarray(x).astype(np.float64)


def striped(idx):
    return np.tile(np.asarray(idx).reshape(-1, 16).T, (8, 1)).astype(np.uint16)


def unstriped(offs):
    return offs[:16].T.reshape(-1).astype(np.int64)


def striped8(idx):
    return np.asarray(idx).reshape(8, -1, 16).transpose(0, 2, 1).reshape(128, -1).astype(np.uint16)


def unstriped8(offs):
    return offs.reshape(8, 16, -1).transpose(0, 2, 1).reshape(8, -1).astype(np.int64)


def pick8(x, idx, run):
    r = np.arange(len(x))
    return x[r[:, None], idx[r % (8 * run) // run]]


E2M1 = np.array([0.0, 0.5, 1.0, 1.5, 2.0, 3.0, 4.0, 6.0, -0.0, -0.5, -1.0, -1.5, -2.0, -3.0, -4.0, -6.0])


def pack_weight(w, fmt):
    k, n = w.shape
    w = f64(np.asarray(w, np.float32).astype(ml_dtypes.bfloat16)).reshape(k // 32, 32, n)
    amax = np.abs(w).max(1)
    if fmt == "e4m3":
        byte = np.frexp(amax)[1] - 1 + 127 - 7
    else:
        mant, ex = np.frexp(amax / 6.0)
        byte = np.where(mant > 0.5, ex, ex - 1) + 127
    byte = np.clip(np.where(amax > 0, byte, 1), 1, 254)
    scaled = (w * np.exp2(127.0 - byte)[:, None, :]).reshape(k, n).astype(np.float32)
    by_word = np.ascontiguousarray(scaled.reshape(k // 512, 128, 4, n).transpose(0, 1, 3, 2))
    if fmt == "e4m3":
        words = by_word.astype(ml_dtypes.float8_e4m3fn).view(np.uint8)
    else:
        c = by_word.astype(ml_dtypes.float4_e2m1fn).view(np.uint8) & 0xF
        words = (c[..., 0::2] | (c[..., 1::2] << 4)).reshape(k // 512, 128, 2 * n)
    return np.ascontiguousarray(words), np.ascontiguousarray(byte.astype(np.uint8).reshape(k // 512, 16, n))


def unpack_weight(words, scales, fmt):
    g, _, n = scales.shape
    words = np.ascontiguousarray(words).reshape(g, 128, n, -1)
    if fmt == "e4m3":
        vals = words.view(ml_dtypes.float8_e4m3fn).astype(np.float64)
    else:
        nib = np.empty((g, 128, n, 4), np.uint8)
        nib[..., 0::2] = words & 0xF
        nib[..., 1::2] = words >> 4
        vals = E2M1[nib]
    vals = vals * np.repeat(np.exp2(scales.astype(np.float64) - 127.0), 8, axis=1)[..., None]
    return vals.transpose(0, 1, 3, 2).reshape(g * 512, n)


K, J, R, T, F, C, O, N, S, Z = 512, 512, 512, 2048, 1024, 1024, 256, 256, 512, 1024


def setup_inputs():
    n = np.random.standard_normal
    idx = np.stack([np.random.permutation(T)[:J] for _ in range(8)])
    idx2 = np.stack([np.random.permutation(T)[:J] for _ in range(8)])
    idx3 = np.random.permutation(F)[:R]
    idx4 = np.random.permutation(C)[:J]
    idx5 = np.random.permutation(C)[:O]
    idx6 = np.stack([np.random.permutation(C)[:O] for _ in range(8)])
    idx7 = np.random.permutation(Z)[:O]
    fk = mx_kscale(K)
    fr = mx_kscale(R)
    fs = mx_kscale(S)
    tr = np.ones(F)
    tr[idx3] = fr
    wtp = pack_weight(n((K, F)) * 1 / np.sqrt(K) / fk[:, None] * tr, "e4m3")
    wbp = pack_weight(n((R, N)) * 1 / np.sqrt(R) / fr[:, None], "e2m1")
    xrp = pack_weight(n((S, Z)) / fs[:, None], "e4m3")
    wsp = pack_weight(n((S, N)) * 1 / np.sqrt(S) * fs[:, None], "e4m3")
    return {
        "ta": (np.random.randint(-7, 8, (K, T)).astype(np.float64)).astype(np.float32),
        "ga": ((np.random.randint(8, 19, (K, 1)) / 64.0) * fk[:, None]).astype(np.float32),
        "gb": ((np.random.randint(8, 19, (K, 1)) / 64.0) * fk[:, None]).astype(np.float32),
        "wt_words": wtp[0],
        "wt_scales": wtp[1],
        "sa": (np.random.uniform(0.5, 1.6, (R, 1))).astype(np.float32),
        "sb": (np.random.uniform(0.5, 1.6, (R, 1))).astype(np.float32),
        "wb_words": wbp[0],
        "wb_scales": wbp[1],
        "xr_words": xrp[0],
        "xr_scales": xrp[1],
        "ws_words": wsp[0],
        "ws_scales": wsp[1],
        "offs": striped8(idx),
        "offs2": striped8(idx2),
        "offs3": striped(idx3),
        "offs4": striped(idx4),
        "offs5": striped(idx5),
        "offs6": striped8(idx6),
        "offs7": striped(idx7),
    }


def reference(ta, ga, gb, wt_words, wt_scales, sa, sb, wb_words, wb_scales, xr_words, xr_scales, ws_words, ws_scales, offs, offs2, offs3, offs4, offs5, offs6, offs7):
    idx = unstriped8(offs)
    idx2 = unstriped8(offs2)
    idx3 = unstriped(offs3)
    idx4 = unstriped(offs4)
    idx5 = unstriped(offs5)
    idx6 = unstriped8(offs6)
    idx7 = unstriped(offs7)
    wtu = unpack_weight(wt_words, wt_scales, "e4m3")
    wbu = unpack_weight(wb_words, wb_scales, "e2m1")
    xru = unpack_weight(xr_words, xr_scales, "e4m3")
    wsu = unpack_weight(ws_words, ws_scales, "e4m3")
    xc = pick8(f64(ta), idx, 64) * f64(ga) - pick8(f64(ta), idx2, 64) * f64(gb)
    wtidx3g = wtu[:, idx3]
    xcq = mxq(xc, 0, "e4m3")
    a = wtidx3g.T @ xcq
    pw = np.zeros((R, C))
    pw[:, idx4] = a
    hid = np.maximum(pw[:, idx5] * f64(sa), pick8(pw, idx6, 64) * f64(sb))
    hidq = mxq(hid, 0, "e4m3")
    xridx7g = xru[:, idx7]
    y = wbu.T @ hidq + wsu.T @ xridx7g
    return y

@@ -1,0 +1,275 @@
+from contextlib import ExitStack
+
+import concourse.mybir as mybir
+
+K, J, R, T, F, C, O, N, S, Z = 512, 512, 512, 2048, 1024, 1024, 256, 256, 512, 1024
+FLOPS = 2 * K * R * J + 2 * R * N * O + 2 * S * N * O
+
+F32 = mybir.dt.float32
+BF16 = mybir.dt.bfloat16
+I32 = mybir.dt.int32
+U32 = mybir.dt.uint32
+U16 = mybir.dt.uint16
+U8 = mybir.dt.uint8
+FP8X4 = mybir.dt.float8_e4m3fn_x4
+FP4X4 = mybir.dt.float4_e2m1fn_x4
+COPY = mybir.ActivationFunctionType.Copy
+SUB = mybir.AluOpType.subtract
+MAX = mybir.AluOpType.max
+
+P = 128
+PACK = 4
+UNIT = 128
+CHUNKS = ((0, 128), (128, 256), (256, 512))
+HALVES = ((0, 128), (128, 256))
+SHARE3 = 224
+
+
+def tile_picked_codegap_store_one_boardmixed_reminder_plain_kernel(
+    tc, ta, ga, gb, wt_words, wt_scales, sa, sb, wb_words, wb_scales, xr_words, xr_scales, ws_words, ws_scales,
+    offs, offs2, offs3, offs4, offs5, offs6, offs7, out,
+):
+    nc = tc.nc
+    with ExitStack() as ctx:
+        keep = ctx.enter_context(tc.tile_pool(name="keep", bufs=1))
+        psum = ctx.enter_context(tc.psum_pool(name="psum", bufs=1))
+
+        def load_list(name, src):
+            tile = keep.tile(list(src.shape), U16, name=name)
+            nc.sync.dma_start(tile[:], src)
+            return tile
+
+        def load_factor(name, src, queue):
+            tile = keep.tile([P, PACK], F32, name=name)
+            queue.dma_start(tile[:], src.rearrange("(p t) o -> p (t o)", t=PACK))
+            return tile
+
+        def load_words(name, src, dtype, width):
+            tile = keep.tile([P, width], dtype, name=name, align_bytes=64)
+            nc.sync.dma_start(tile[:].bitcast(I32), src.bitcast(I32))
+            return tile
+
+        def zeroed_plane(name, width):
+            tile = keep.tile([P, width], U8, name=name, align_bytes=64)
+            nc.vector.memset(tile[:].bitcast(I32), 0)
+            return tile
+
+        def load_plane(tile, src):
+            for q in range(4):
+                nc.sync.dma_start(tile[32 * q : 32 * q + 4, :].bitcast(I32), src[0, 4 * q : 4 * q + 4, :].bitcast(I32))
+
+        def load_rows(name, src, width):
+            tile = keep.tile([P, 2, width // 4], I32, name=name)
+            for half in range(2):
+                rows = src[0, 8 * half : 8 * half + 8, :].rearrange("(q i) w -> i q w", i=4)
+                nc.sync.dma_start(tile[64 * half : 64 * half + 4], rows.bitcast(I32))
+            return tile
+
+        def spread_rows(plane, rows):
+            for q in range(4):
+                first_row = 64 * (q // 2)
+                nc.vector.tensor_copy(plane[32 * q : 32 * q + 4, :].bitcast(I32), rows[first_row : first_row + 4, q % 2, :])
+
+        wt_plane = zeroed_plane("wt_plane", F)
+        xr_plane = zeroed_plane("xr_plane", Z)
+        ws_plane = zeroed_plane("ws_plane", N)
+        wb_plane = zeroed_plane("wb_plane", N)
+        board = [keep.tile([P, C], F32, name="board%d" % t) for t in range(PACK)]
+        for t in range(PACK):
+            nc.vector.memset(board[t][:], 0.0)
+
+        ta_rows = ta.rearrange("(p t) c -> t p c", t=PACK)
+        table = [keep.tile([P, T], F32, name="table%d" % t) for t in range(PACK)]
+        list1 = load_list("list1", offs)
+        step_a = load_factor("step_a", ga, nc.scalar)
+        nc.sync.dma_start(table[0][:], ta_rows[0])
+        list2 = load_list("list2", offs2)
+        step_b = load_factor("step_b", gb, nc.scalar)
+        nc.sync.dma_start(table[1][:], ta_rows[1])
+        list3 = load_list("list3", offs3)
+        wt_rows = load_rows("wt_rows", wt_scales, F)
+        nc.sync.dma_start(table[2][:], ta_rows[2])
+        nc.sync.dma_start(table[3][:], ta_rows[3])
+        wt_store = load_words("wt_store", wt_words[0].rearrange("p c r -> p (c r)"), U32, F)
+        list4 = load_list("list4", offs4)
+        list7 = load_list("list7", offs7)
+        xr_store = load_words("xr_store", xr_words[0].rearrange("p c r -> p (c r)"), U32, Z)
+        load_plane(xr_plane, xr_scales)
+        list5 = load_list("list5", offs5)
+        list6 = load_list("list6", offs6)
+        weight_a = load_factor("weight_a", sa, nc.sync)
+        weight_b = load_factor("weight_b", sb, nc.sync)
+        ws_codes = load_words("ws_codes", ws_words[0].rearrange("p c r -> p (c r)"), U32, N)
+        load_plane(ws_plane, ws_scales)
+        wb_codes = load_words("wb_codes", wb_words[0], U8, 2 * N)
+        load_plane(wb_plane, wb_scales)
+
+        first = [keep.tile([P, 2, J], F32, name="first%d" % u) for u in range(2)]
+        second = [keep.tile([P, 2, J], F32, name="second%d" % u) for u in range(2)]
+        for t in range(PACK):
+            nc.scalar.activation(first[t // 2][:, t % 2, :], table[t][:].indirect(list1[:]), COPY, scale=step_a[:, t : t + 1])
+            nc.scalar.activation(second[t // 2][:, t % 2, :], table[t][:].indirect(list2[:]), COPY, scale=step_b[:, t : t + 1])
+
+        spread_rows(wt_plane, wt_rows)
+        wt_codes = keep.tile([P, R], U32, name="wt_codes", align_bytes=64)
+        wt_bytes = keep.tile([P, R], U8, name="wt_bytes", align_bytes=64)
+
+        nc.vector.tensor_copy(wt_bytes[:].rearrange("p (t m) -> p m t", t=PACK), wt_plane[:].indirect(list3[:]))
+
+        def combine(pairs, t, left, right, op, lo, hi):
+            nc.vector.tensor_tensor(
+                pairs[:, lo // UNIT : hi // UNIT, t // 2, :, t % 2],
+                left[t // 2][:, t % 2, lo:hi].rearrange("p (c j) -> p c j", j=UNIT),
+                right[t // 2][:, t % 2, lo:hi].rearrange("p (c j) -> p c j", j=UNIT),
+                op,
+            )
+
+        def combine_first_pair(pairs, left, right, op):
+            nc.vector.tensor_tensor(
+                pairs[:, :, 0],
+                left[0][:].rearrange("p e (c j) -> p c j e", j=UNIT),
+                right[0][:].rearrange("p e (c j) -> p c j e", j=UNIT),
+                op,
+            )
+
+        def weave(engine_copy, word, dst, pairs, lo, hi):
+            words = pairs[:, lo // UNIT : hi // UNIT].rearrange("p c u j e -> p c u (j e)").bitcast(word)
+            engine_copy(
+                dst[:].bitcast(word).rearrange("p (c j u) -> p c j u", j=UNIT, u=2), words.rearrange("p c u j -> p c j u")
+            )
+
+        xc_pairs = keep.tile([P, J // UNIT, 2, UNIT, 2], BF16, name="xc_pairs")
+        xc = [keep.tile([P, (hi - lo) * PACK], BF16, name="xc%d" % lo, align_bytes=64) for lo, hi in CHUNKS]
+
+        def subtract(t, lo, hi):
+            combine(xc_pairs, t, first, second, SUB, lo, hi)
+
+        combine_first_pair(xc_pairs, first, second, SUB)
+        subtract(2, 0, J)
+        nc.vector.tensor_copy(wt_codes[:].rearrange("p (t m) -> p m t", t=PACK), wt_store[:].indirect(list3[:]))
+
+        hidden = keep.tile([P, PACK, J], F32, name="hidden")
+        banks = {}
+
+        def quantise_multiply(c, groups):
+            lo, hi = CHUNKS[c]
+            width = hi - lo
+            codes = keep.tile([P, width], U32, name="xc_codes%d" % c, align_bytes=64)
+            plane = keep.tile([P, width], U8, name="xc_plane%d" % c, align_bytes=64)
+            nc.vector.quantize_mx(out=codes[:].bitcast(FP8X4), scales=plane[:], in_=xc[c][:])
+            for t0, t1 in groups:
+                bank = psum.tile([P, t1 - t0, width], F32, name="bank%d_%d" % (c, t0))
+                banks[c, t0] = bank
+                for t in range(t0, t1):
+                    nc.tensor.matmul_mx(
+                        out=bank[:, t - t0, :],
+                        lhsT=wt_codes[:, t * P : (t + 1) * P].bitcast(FP8X4),
+                        lhsT_scale=wt_bytes[:, t * P : (t + 1) * P],
+                        rhs=codes[:].bitcast(FP8X4),
+                        rhs_scale=plane[:],
+                        start=True,
+                        stop=True,
+                    )
+
+        for c, (lo, hi) in enumerate(CHUNKS):
+            subtract(3, lo, hi)
+            weave(nc.scalar.copy, U32, xc[c], xc_pairs, lo, hi)
+        quantise_multiply(0, ((0, 1), (1, 4)))
+        quantise_multiply(1, ((0, 4),))
+        quantise_multiply(2, ((0, 2), (2, 4)))
+
+        def empty(engine_copy, c, t0):
+            lo, hi = CHUNKS[c]
+            bank = banks[c, t0]
+            engine_copy(hidden[:, t0 : t0 + bank.shape[1], lo:hi], bank[:])
+
+        def put_vector(t, lo, hi):
+            nc.vector.tensor_copy(board[t][:].indirect(list4[:, lo // 16 : hi // 16]), hidden[:, t, lo:hi])
+
+        def put_scalar(t, lo, hi):
+            nc.scalar.activation(board[t][:].indirect(list4[:, lo // 16 : hi // 16]), hidden[:, t, lo:hi], COPY)
+
+        read_a = [keep.tile([P, 2, O], F32, name="read_a%d" % u) for u in range(2)]
+        read_b = [keep.tile([P, 2, O], F32, name="read_b%d" % u) for u in range(2)]
+
+        def fetch_a(t, lo, hi):
+            nc.scalar.activation(
+                read_a[t // 2][:, t % 2, lo:hi], board[t][:].indirect(list5[:, lo // 16 : hi // 16]), COPY, scale=weight_a[:, t : t + 1]
+            )
+
+        def fetch_b(t):
+            nc.scalar.activation(read_b[t // 2][:, t % 2, :], board[t][:].indirect(list6[:]), COPY, scale=weight_b[:, t : t + 1])
+
+        def fetch(t):
+            fetch_a(t, 0, O)
+            fetch_b(t)
+
+        empty(nc.scalar.copy, 0, 0)
+        put_scalar(0, 0, 128)
+        empty(nc.vector.tensor_copy, 0, 1)
+        put_vector(1, 0, 128)
+        empty(nc.scalar.copy, 1, 0)
+        put_vector(2, 0, 128)
+        empty(nc.scalar.copy, 2, 0)
+        empty(nc.scalar.copy, 2, 2)
+        put_scalar(0, 128, 512)
+        put_vector(1, 128, 512)
+        put_scalar(3, 0, SHARE3)
+        put_vector(2, 128, 512)
+        put_vector(3, SHARE3, 512)
+        for t in range(PACK - 1):
+            fetch(t)
+        fetch_b(3)
+        for lo, hi in HALVES:
+            fetch_a(3, lo, hi)
+
+        xr_codes = keep.tile([P, O], U32, name="xr_codes", align_bytes=64)
+        xr_bytes = keep.tile([P, O], U8, name="xr_bytes", align_bytes=64)
+        nc.vector.tensor_copy(xr_codes[:], xr_store[:].indirect(list7[:]))
+        nc.vector.tensor_copy(xr_bytes[:], xr_plane[:].indirect(list7[:]))
+        sums = [psum.tile([P, O], F32, name="sums%d" % h) for h in range(2)]
+        for h in range(2):
+            nc.tensor.matmul_mx(
+                out=sums[h][:],
+                lhsT=ws_codes[:, h * P : (h + 1) * P].bitcast(FP8X4),
+                lhsT_scale=ws_plane[:, h * P : (h + 1) * P],
+                rhs=xr_codes[:].bitcast(FP8X4),
+                rhs_scale=xr_bytes[:],
+                start=True,
+                stop=False,
+            )
+
+        hid_pairs = keep.tile([P, O // UNIT, 2, UNIT, 2], BF16, name="hid_pairs")
+        hid = [keep.tile([P, UNIT * PACK], BF16, name="hid%d" % lo, align_bytes=64) for lo, hi in HALVES]
+
+        def larger(t, lo, hi):
+            combine(hid_pairs, t, read_a, read_b, MAX, lo, hi)
+
+        def finish(g):
+            lo, hi = HALVES[g]
+            codes = keep.tile([P, UNIT], U32, name="hid_codes%d" % g, align_bytes=64)
+            plane = keep.tile([P, UNIT], U8, name="hid_plane%d" % g, align_bytes=64)
+            nc.vector.quantize_mx(out=codes[:].bitcast(FP8X4), scales=plane[:], in_=hid[g][:])
+            for h in range(2):
+                nc.tensor.matmul_mx(
+                    out=sums[h][:, lo:hi],
+                    lhsT=wb_codes[:, 2 * h * P : 2 * (h + 1) * P].bitcast(FP4X4),
+                    lhsT_scale=wb_plane[:, h * P : (h + 1) * P],
+                    rhs=codes[:].bitcast(FP8X4),
+                    rhs_scale=plane[:],
+                    start=False,
+                    stop=(g == len(HALVES) - 1),
+                )
+
+        combine_first_pair(hid_pairs, read_a, read_b, MAX)
+        larger(2, 0, O)
+        larger(3, *HALVES[0])
+        weave(nc.vector.tensor_copy, I32, hid[0], hid_pairs, *HALVES[0])
+        larger(3, *HALVES[1])
+        finish(0)
+        weave(nc.vector.tensor_copy, I32, hid[1], hid_pairs, *HALVES[1])
+        finish(1)
+        for h, (engine_copy, queue) in enumerate(((nc.vector.tensor_copy, nc.sync), (nc.scalar.copy, nc.scalar))):
+            result = keep.tile([P, O], F32, name="result%d" % h)
+            engine_copy(result[:], sums[h][:])
+            queue.dma_start(out[h * P : (h + 1) * P, :], result[:])

@@ -71,6 +71,10 @@ def tile_picked_codegap_store_one_boardmixed_reminder_plain_kernel(
                 nc.vector.tensor_copy(plane[32 * q : 32 * q + 4, :].bitcast(I32), rows[first_row : first_row + 4, q % 2, :])
 
         wt_plane = zeroed_plane("wt_plane", F)
+        warm_in = keep.tile([P, 1], F32, name="warm_in")
+        warm_out = keep.tile([P, 1], F32, name="warm_out")
+        nc.gpsimd.memset(warm_in[:], 0.0)
+        nc.scalar.activation(warm_out[:], warm_in[:], COPY)
         xr_plane = zeroed_plane("xr_plane", Z)
         ws_plane = zeroed_plane("ws_plane", N)
         wb_plane = zeroed_plane("wb_plane", N)

@@ -20,9 +20,10 @@ MAX = mybir.AluOpType.max
 P = 128
 PACK = 4
 UNIT = 128
-CHUNKS = ((0, 128), (128, 256), (256, 512))
+CHUNKS = ((0, 256), (256, 512))
+PIECES = ((0, 128), (128, 256), (256, 512))
 HALVES = ((0, 128), (128, 256))
-SHARE3 = 224
+SHARE3 = 288
 
 
 def tile_picked_codegap_store_one_boardmixed_reminder_plain_kernel(
@@ -49,8 +50,8 @@ def tile_picked_codegap_store_one_boardmixed_reminder_plain_kernel(
             nc.sync.dma_start(tile[:].bitcast(I32), src.bitcast(I32))
             return tile
 
-        def zeroed_plane(name, width):
-            tile = keep.tile([P, width], U8, name=name, align_bytes=64)
+        def zeroed_plane(name, width, tag):
+            tile = keep.tile([P, width], U8, name=name, tag=tag, align_bytes=64)
             nc.vector.memset(tile[:].bitcast(I32), 0)
             return tile
 
@@ -70,14 +71,14 @@ def tile_picked_codegap_store_one_boardmixed_reminder_plain_kernel(
                 first_row = 64 * (q // 2)
                 nc.vector.tensor_copy(plane[32 * q : 32 * q + 4, :].bitcast(I32), rows[first_row : first_row + 4, q % 2, :])
 
-        wt_plane = zeroed_plane("wt_plane", F)
+        wt_plane = zeroed_plane("wt_plane", F, "wt_plane_then_pairs")
         warm_in = keep.tile([P, 1], F32, name="warm_in")
         warm_out = keep.tile([P, 1], F32, name="warm_out")
         nc.gpsimd.memset(warm_in[:], 0.0)
         nc.scalar.activation(warm_out[:], warm_in[:], COPY)
-        xr_plane = zeroed_plane("xr_plane", Z)
-        ws_plane = zeroed_plane("ws_plane", N)
-        wb_plane = zeroed_plane("wb_plane", N)
+        xr_plane = zeroed_plane("xr_plane", Z, "xr_plane")
+        ws_plane = zeroed_plane("ws_plane", N, "ws_plane")
+        wb_plane = zeroed_plane("wb_plane", N, "wb_plane")
         board = [keep.tile([P, C], F32, name="board%d" % t) for t in range(PACK)]
         for t in range(PACK):
             nc.vector.memset(board[t][:], 0.0)
@@ -120,78 +121,64 @@ def tile_picked_codegap_store_one_boardmixed_reminder_plain_kernel(
 
         nc.vector.tensor_copy(wt_bytes[:].rearrange("p (t m) -> p m t", t=PACK), wt_plane[:].indirect(list3[:]))
 
-        def combine(pairs, t, left, right, op, lo, hi):
+        def combine(pairs, u, left, right, op, lo, hi):
             nc.vector.tensor_tensor(
-                pairs[:, lo // UNIT : hi // UNIT, t // 2, :, t % 2],
-                left[t // 2][:, t % 2, lo:hi].rearrange("p (c j) -> p c j", j=UNIT),
-                right[t // 2][:, t % 2, lo:hi].rearrange("p (c j) -> p c j", j=UNIT),
-                op,
-            )
-
-        def combine_first_pair(pairs, left, right, op):
-            nc.vector.tensor_tensor(
-                pairs[:, :, 0],
-                left[0][:].rearrange("p e (c j) -> p c j e", j=UNIT),
-                right[0][:].rearrange("p e (c j) -> p c j e", j=UNIT),
+                pairs[:, u, lo:hi, :],
+                left[u][:, :, lo:hi].rearrange("p e j -> p j e"),
+                right[u][:, :, lo:hi].rearrange("p e j -> p j e"),
                 op,
             )
 
         def weave(engine_copy, word, dst, pairs, lo, hi):
-            words = pairs[:, lo // UNIT : hi // UNIT].rearrange("p c u j e -> p c u (j e)").bitcast(word)
-            engine_copy(
-                dst[:].bitcast(word).rearrange("p (c j u) -> p c j u", j=UNIT, u=2), words.rearrange("p c u j -> p c j u")
-            )
+            words = pairs[:].rearrange("p u j e -> p u (j e)").bitcast(word)
+            engine_copy(dst.bitcast(word).rearrange("p (j u) -> p j u", u=2), words[:, :, lo:hi].rearrange("p u j -> p j u"))
 
-        xc_pairs = keep.tile([P, J // UNIT, 2, UNIT, 2], BF16, name="xc_pairs")
+        xc_pairs = keep.tile([P, 2, J, 2], BF16, name="xc_pairs", tag="wt_plane_then_pairs", align_bytes=64)
         xc = [keep.tile([P, (hi - lo) * PACK], BF16, name="xc%d" % lo, align_bytes=64) for lo, hi in CHUNKS]
 
-        def subtract(t, lo, hi):
-            combine(xc_pairs, t, first, second, SUB, lo, hi)
-
-        combine_first_pair(xc_pairs, first, second, SUB)
-        subtract(2, 0, J)
+        combine(xc_pairs, 0, first, second, SUB, 0, J)
         nc.vector.tensor_copy(wt_codes[:].rearrange("p (t m) -> p m t", t=PACK), wt_store[:].indirect(list3[:]))
 
-        hidden = keep.tile([P, PACK, J], F32, name="hidden")
         banks = {}
 
-        def quantise_multiply(c, groups):
+        def quantise_multiply(c):
             lo, hi = CHUNKS[c]
             width = hi - lo
             codes = keep.tile([P, width], U32, name="xc_codes%d" % c, align_bytes=64)
             plane = keep.tile([P, width], U8, name="xc_plane%d" % c, align_bytes=64)
             nc.vector.quantize_mx(out=codes[:].bitcast(FP8X4), scales=plane[:], in_=xc[c][:])
-            for t0, t1 in groups:
-                bank = psum.tile([P, t1 - t0, width], F32, name="bank%d_%d" % (c, t0))
-                banks[c, t0] = bank
-                for t in range(t0, t1):
-                    nc.tensor.matmul_mx(
-                        out=bank[:, t - t0, :],
-                        lhsT=wt_codes[:, t * P : (t + 1) * P].bitcast(FP8X4),
-                        lhsT_scale=wt_bytes[:, t * P : (t + 1) * P],
-                        rhs=codes[:].bitcast(FP8X4),
-                        rhs_scale=plane[:],
-                        start=True,
-                        stop=True,
-                    )
+            for t in range(PACK):
+                banks[t, c] = psum.tile([P, width], F32, name="bank%d_%d" % (t, c), tag="bank%d_%d" % (t, c))
+                nc.tensor.matmul_mx(
+                    out=banks[t, c][:],
+                    lhsT=wt_codes[:, t * P : (t + 1) * P].bitcast(FP8X4),
+                    lhsT_scale=wt_bytes[:, t * P : (t + 1) * P],
+                    rhs=codes[:].bitcast(FP8X4),
+                    rhs_scale=plane[:],
+                    start=True,
+                    stop=True,
+                )
 
-        for c, (lo, hi) in enumerate(CHUNKS):
-            subtract(3, lo, hi)
-            weave(nc.scalar.copy, U32, xc[c], xc_pairs, lo, hi)
-        quantise_multiply(0, ((0, 1), (1, 4)))
-        quantise_multiply(1, ((0, 4),))
-        quantise_multiply(2, ((0, 2), (2, 4)))
-
-        def empty(engine_copy, c, t0):
-            lo, hi = CHUNKS[c]
-            bank = banks[c, t0]
-            engine_copy(hidden[:, t0 : t0 + bank.shape[1], lo:hi], bank[:])
+        for lo, hi in PIECES:
+            c = lo // 256
+            combine(xc_pairs, 1, first, second, SUB, lo, hi)
+            weave(nc.scalar.copy, U32, xc[c][:, PACK * (lo - 256 * c) : PACK * (hi - 256 * c)], xc_pairs, lo, hi)
+        for c in range(len(CHUNKS)):
+            quantise_multiply(c)
 
         def put_vector(t, lo, hi):
-            nc.vector.tensor_copy(board[t][:].indirect(list4[:, lo // 16 : hi // 16]), hidden[:, t, lo:hi])
+            c = lo // 256
+            values = keep.tile([P, hi - lo], F32, name="values", tag="ring", bufs=2, align_bytes=64)
+            nc.vector.tensor_copy(values[:], banks[t, c][:, lo - 256 * c : hi - 256 * c])
+            nc.vector.tensor_copy(board[t][:].indirect(list4[:, lo // 16 : hi // 16]), values[:])
 
         def put_scalar(t, lo, hi):
-            nc.scalar.activation(board[t][:].indirect(list4[:, lo // 16 : hi // 16]), hidden[:, t, lo:hi], COPY)
+            values = keep.tile([P, hi - lo], F32, name="values%d_%d" % (t, lo))
+            for c, (c_lo, c_hi) in enumerate(CHUNKS):
+                a, b = max(lo, c_lo), min(hi, c_hi)
+                if a < b:
+                    nc.scalar.copy(values[:, a - lo : b - lo], banks[t, c][:, a - c_lo : b - c_lo])
+            nc.scalar.activation(board[t][:].indirect(list4[:, lo // 16 : hi // 16]), values[:], COPY)
 
         read_a = [keep.tile([P, 2, O], F32, name="read_a%d" % u) for u in range(2)]
         read_b = [keep.tile([P, 2, O], F32, name="read_b%d" % u) for u in range(2)]
@@ -208,30 +195,23 @@ def tile_picked_codegap_store_one_boardmixed_reminder_plain_kernel(
             fetch_a(t, 0, O)
             fetch_b(t)
 
-        empty(nc.scalar.copy, 0, 0)
-        put_scalar(0, 0, 128)
-        empty(nc.vector.tensor_copy, 0, 1)
-        put_vector(1, 0, 128)
-        empty(nc.scalar.copy, 1, 0)
-        put_vector(2, 0, 128)
-        empty(nc.scalar.copy, 2, 0)
-        empty(nc.scalar.copy, 2, 2)
-        put_scalar(0, 128, 512)
-        put_vector(1, 128, 512)
+        for lo, hi in CHUNKS:
+            put_scalar(0, lo, hi)
+            put_vector(1, lo, hi)
+            put_vector(2, lo, hi)
         put_scalar(3, 0, SHARE3)
-        put_vector(2, 128, 512)
-        put_vector(3, SHARE3, 512)
+        put_vector(3, SHARE3, J)
         for t in range(PACK - 1):
             fetch(t)
         fetch_b(3)
         for lo, hi in HALVES:
             fetch_a(3, lo, hi)
 
-        xr_codes = keep.tile([P, O], U32, name="xr_codes", align_bytes=64)
-        xr_bytes = keep.tile([P, O], U8, name="xr_bytes", align_bytes=64)
+        xr_codes = keep.tile([P, O], U32, name="xr_codes", tag="ring", bufs=2, align_bytes=64)
+        xr_bytes = keep.tile([P, O], U8, name="xr_bytes", tag="ring", bufs=2, align_bytes=64)
         nc.vector.tensor_copy(xr_codes[:], xr_store[:].indirect(list7[:]))
         nc.vector.tensor_copy(xr_bytes[:], xr_plane[:].indirect(list7[:]))
-        sums = [psum.tile([P, O], F32, name="sums%d" % h) for h in range(2)]
+        sums = [psum.tile([P, O], F32, name="sums%d" % h, tag="bank%d_0" % (h + 1)) for h in range(2)]
         for h in range(2):
             nc.tensor.matmul_mx(
                 out=sums[h][:],
@@ -243,11 +223,11 @@ def tile_picked_codegap_store_one_boardmixed_reminder_plain_kernel(
                 stop=False,
             )
 
-        hid_pairs = keep.tile([P, O // UNIT, 2, UNIT, 2], BF16, name="hid_pairs")
+        hid_pairs = keep.tile([P, 2, O, 2], BF16, name="hid_pairs")
         hid = [keep.tile([P, UNIT * PACK], BF16, name="hid%d" % lo, align_bytes=64) for lo, hi in HALVES]
 
-        def larger(t, lo, hi):
-            combine(hid_pairs, t, read_a, read_b, MAX, lo, hi)
+        def larger(u, lo, hi):
+            combine(hid_pairs, u, read_a, read_b, MAX, lo, hi)
 
         def finish(g):
             lo, hi = HALVES[g]
@@ -265,13 +245,12 @@ def tile_picked_codegap_store_one_boardmixed_reminder_plain_kernel(
                     stop=(g == len(HALVES) - 1),
                 )
 
-        combine_first_pair(hid_pairs, read_a, read_b, MAX)
-        larger(2, 0, O)
-        larger(3, *HALVES[0])
-        weave(nc.vector.tensor_copy, I32, hid[0], hid_pairs, *HALVES[0])
-        larger(3, *HALVES[1])
+        larger(0, 0, O)
+        larger(1, *HALVES[0])
+        weave(nc.vector.tensor_copy, I32, hid[0][:], hid_pairs, *HALVES[0])
+        larger(1, *HALVES[1])
         finish(0)
-        weave(nc.vector.tensor_copy, I32, hid[1], hid_pairs, *HALVES[1])
+        weave(nc.vector.tensor_copy, I32, hid[1][:], hid_pairs, *HALVES[1])
         finish(1)
         for h, (engine_copy, queue) in enumerate(((nc.vector.tensor_copy, nc.sync), (nc.scalar.copy, nc.scalar))):
             result = keep.tile([P, O], F32, name="result%d" % h)

@@ -23,7 +23,7 @@ UNIT = 128
 CHUNKS = ((0, 256), (256, 512))
 PIECES = ((0, 128), (128, 256), (256, 512))
 HALVES = ((0, 128), (128, 256))
-SHARE3 = 288
+SHARE3 = 320
 
 
 def tile_picked_codegap_store_one_boardmixed_reminder_plain_kernel(
@@ -211,48 +211,53 @@ def tile_picked_codegap_store_one_boardmixed_reminder_plain_kernel(
         xr_bytes = keep.tile([P, O], U8, name="xr_bytes", tag="ring", bufs=2, align_bytes=64)
         nc.vector.tensor_copy(xr_codes[:], xr_store[:].indirect(list7[:]))
         nc.vector.tensor_copy(xr_bytes[:], xr_plane[:].indirect(list7[:]))
-        sums = [psum.tile([P, O], F32, name="sums%d" % h, tag="bank%d_0" % (h + 1)) for h in range(2)]
-        for h in range(2):
-            nc.tensor.matmul_mx(
-                out=sums[h][:],
-                lhsT=ws_codes[:, h * P : (h + 1) * P].bitcast(FP8X4),
-                lhsT_scale=ws_plane[:, h * P : (h + 1) * P],
-                rhs=xr_codes[:].bitcast(FP8X4),
-                rhs_scale=xr_bytes[:],
-                start=True,
-                stop=False,
+        sums = {}
+        for g, (lo, hi) in enumerate(HALVES):
+            for h in range(2):
+                sums[g, h] = psum.tile([P, UNIT], F32, name="sums%d_%d" % (g, h), tag="bank%d_%d" % (h + 1, g))
+                nc.tensor.matmul_mx(
+                    out=sums[g, h][:],
+                    lhsT=ws_codes[:, h * P : (h + 1) * P].bitcast(FP8X4),
+                    lhsT_scale=ws_plane[:, h * P : (h + 1) * P],
+                    rhs=xr_codes[:, lo:hi].bitcast(FP8X4),
+                    rhs_scale=xr_bytes[:, lo:hi],
+                    start=True,
+                    stop=False,
+                )
+
+        hid = [keep.tile([P, UNIT, PACK], BF16, name="hid%d" % lo, align_bytes=64) for lo, hi in HALVES]
+
+        def larger(u, g):
+            lo, hi = HALVES[g]
+            nc.vector.tensor_tensor(
+                hid[g][:, :, 2 * u : 2 * u + 2],
+                read_a[u][:, :, lo:hi].rearrange("p e o -> p o e"),
+                read_b[u][:, :, lo:hi].rearrange("p e o -> p o e"),
+                MAX,
             )
 
-        hid_pairs = keep.tile([P, 2, O, 2], BF16, name="hid_pairs")
-        hid = [keep.tile([P, UNIT * PACK], BF16, name="hid%d" % lo, align_bytes=64) for lo, hi in HALVES]
-
-        def larger(u, lo, hi):
-            combine(hid_pairs, u, read_a, read_b, MAX, lo, hi)
-
-        def finish(g):
+        def finish(g, ways_out):
             lo, hi = HALVES[g]
             codes = keep.tile([P, UNIT], U32, name="hid_codes%d" % g, align_bytes=64)
             plane = keep.tile([P, UNIT], U8, name="hid_plane%d" % g, align_bytes=64)
-            nc.vector.quantize_mx(out=codes[:].bitcast(FP8X4), scales=plane[:], in_=hid[g][:])
+            nc.vector.quantize_mx(out=codes[:].bitcast(FP8X4), scales=plane[:], in_=hid[g][:].rearrange("p o t -> p (o t)"))
             for h in range(2):
                 nc.tensor.matmul_mx(
-                    out=sums[h][:, lo:hi],
+                    out=sums[g, h][:],
                     lhsT=wb_codes[:, 2 * h * P : 2 * (h + 1) * P].bitcast(FP4X4),
                     lhsT_scale=wb_plane[:, h * P : (h + 1) * P],
                     rhs=codes[:].bitcast(FP8X4),
                     rhs_scale=plane[:],
                     start=False,
-                    stop=(g == len(HALVES) - 1),
+                    stop=True,
                 )
+            for h, (engine_copy, queue) in enumerate(ways_out):
+                result = keep.tile([P, UNIT], F32, name="result%d_%d" % (g, h))
+                engine_copy(result[:], sums[g, h][:])
+                queue.dma_start(out[h * P : (h + 1) * P, lo:hi], result[:])
 
-        larger(0, 0, O)
-        larger(1, *HALVES[0])
-        weave(nc.vector.tensor_copy, I32, hid[0][:], hid_pairs, *HALVES[0])
-        larger(1, *HALVES[1])
-        finish(0)
-        weave(nc.vector.tensor_copy, I32, hid[1][:], hid_pairs, *HALVES[1])
-        finish(1)
-        for h, (engine_copy, queue) in enumerate(((nc.vector.tensor_copy, nc.sync), (nc.scalar.copy, nc.scalar))):
-            result = keep.tile([P, O], F32, name="result%d" % h)
-            engine_copy(result[:], sums[h][:])
-            queue.dma_start(out[h * P : (h + 1) * P, :], result[:])
+        for u in range(2):
+            for g in range(len(HALVES)):
+                larger(u, g)
+        finish(0, ((nc.scalar.copy, nc.sync), (nc.scalar.copy, nc.sync)))
+        finish(1, ((nc.vector.tensor_copy, nc.sync), (nc.scalar.copy, nc.scalar)))

from contextlib import ExitStack

import concourse.mybir as mybir

K, J, R, T, F, C, O, N, S, Z = 512, 512, 512, 2048, 1024, 1024, 256, 256, 512, 1024
FLOPS = 2 * K * R * J + 2 * R * N * O + 2 * S * N * O

F32 = mybir.dt.float32
BF16 = mybir.dt.bfloat16
I32 = mybir.dt.int32
U32 = mybir.dt.uint32
U16 = mybir.dt.uint16
U8 = mybir.dt.uint8
FP8X4 = mybir.dt.float8_e4m3fn_x4
FP4X4 = mybir.dt.float4_e2m1fn_x4
COPY = mybir.ActivationFunctionType.Copy
SUB = mybir.AluOpType.subtract
MAX = mybir.AluOpType.max

P = 128
PACK = 4
UNIT = 128
CHUNKS = ((0, 256), (256, 512))
PIECES = ((0, 128), (128, 256), (256, 512))
HALVES = ((0, 128), (128, 256))
SHARE3 = 320


def tile_picked_codegap_store_one_boardmixed_reminder_plain_kernel(
    tc, ta, ga, gb, wt_words, wt_scales, sa, sb, wb_words, wb_scales, xr_words, xr_scales, ws_words, ws_scales,
    offs, offs2, offs3, offs4, offs5, offs6, offs7, out,
):
    nc = tc.nc
    with ExitStack() as ctx:
        keep = ctx.enter_context(tc.tile_pool(name="keep", bufs=1))
        psum = ctx.enter_context(tc.psum_pool(name="psum", bufs=1))

        def load_list(name, src):
            tile = keep.tile(list(src.shape), U16, name=name)
            nc.sync.dma_start(tile[:], src)
            return tile

        def load_factor(name, src, queue):
            tile = keep.tile([P, PACK], F32, name=name)
            queue.dma_start(tile[:], src.rearrange("(p t) o -> p (t o)", t=PACK))
            return tile

        def load_words(name, src, dtype, width):
            tile = keep.tile([P, width], dtype, name=name, align_bytes=64)
            nc.sync.dma_start(tile[:].bitcast(I32), src.bitcast(I32))
            return tile

        def zeroed_plane(name, width, tag):
            tile = keep.tile([P, width], U8, name=name, tag=tag, align_bytes=64)
            nc.vector.memset(tile[:].bitcast(I32), 0)
            return tile

        def load_plane(tile, src):
            for q in range(4):
                nc.sync.dma_start(tile[32 * q : 32 * q + 4, :].bitcast(I32), src[0, 4 * q : 4 * q + 4, :].bitcast(I32))

        def load_rows(name, src, width):
            tile = keep.tile([P, 2, width // 4], I32, name=name)
            for half in range(2):
                rows = src[0, 8 * half : 8 * half + 8, :].rearrange("(q i) w -> i q w", i=4)
                nc.sync.dma_start(tile[64 * half : 64 * half + 4], rows.bitcast(I32))
            return tile

        def spread_rows(plane, rows):
            for q in range(4):
                first_row = 64 * (q // 2)
                nc.vector.tensor_copy(plane[32 * q : 32 * q + 4, :].bitcast(I32), rows[first_row : first_row + 4, q % 2, :])

        wt_plane = zeroed_plane("wt_plane", F, "wt_plane_then_pairs")
        warm_in = keep.tile([P, 1], F32, name="warm_in")
        warm_out = keep.tile([P, 1], F32, name="warm_out")
        nc.gpsimd.memset(warm_in[:], 0.0)
        nc.scalar.activation(warm_out[:], warm_in[:], COPY)
        xr_plane = zeroed_plane("xr_plane", Z, "xr_plane")
        ws_plane = zeroed_plane("ws_plane", N, "ws_plane")
        wb_plane = zeroed_plane("wb_plane", N, "wb_plane")
        board = [keep.tile([P, C], F32, name="board%d" % t) for t in range(PACK)]
        for t in range(PACK):
            nc.vector.memset(board[t][:], 0.0)

        ta_rows = ta.rearrange("(p t) c -> t p c", t=PACK)
        table = [keep.tile([P, T], F32, name="table%d" % t) for t in range(PACK)]
        list1 = load_list("list1", offs)
        step_a = load_factor("step_a", ga, nc.scalar)
        nc.sync.dma_start(table[0][:], ta_rows[0])
        list2 = load_list("list2", offs2)
        step_b = load_factor("step_b", gb, nc.scalar)
        nc.sync.dma_start(table[1][:], ta_rows[1])
        list3 = load_list("list3", offs3)
        wt_rows = load_rows("wt_rows", wt_scales, F)
        nc.sync.dma_start(table[2][:], ta_rows[2])
        nc.sync.dma_start(table[3][:], ta_rows[3])
        wt_store = load_words("wt_store", wt_words[0].rearrange("p c r -> p (c r)"), U32, F)
        list4 = load_list("list4", offs4)
        list7 = load_list("list7", offs7)
        xr_store = load_words("xr_store", xr_words[0].rearrange("p c r -> p (c r)"), U32, Z)
        load_plane(xr_plane, xr_scales)
        list5 = load_list("list5", offs5)
        list6 = load_list("list6", offs6)
        weight_a = load_factor("weight_a", sa, nc.sync)
        weight_b = load_factor("weight_b", sb, nc.sync)
        ws_codes = load_words("ws_codes", ws_words[0].rearrange("p c r -> p (c r)"), U32, N)
        load_plane(ws_plane, ws_scales)
        wb_codes = load_words("wb_codes", wb_words[0], U8, 2 * N)
        load_plane(wb_plane, wb_scales)

        first = [keep.tile([P, 2, J], F32, name="first%d" % u) for u in range(2)]
        second = [keep.tile([P, 2, J], F32, name="second%d" % u) for u in range(2)]
        for t in range(PACK):
            nc.scalar.activation(first[t // 2][:, t % 2, :], table[t][:].indirect(list1[:]), COPY, scale=step_a[:, t : t + 1])
            nc.scalar.activation(second[t // 2][:, t % 2, :], table[t][:].indirect(list2[:]), COPY, scale=step_b[:, t : t + 1])

        spread_rows(wt_plane, wt_rows)
        wt_codes = keep.tile([P, R], U32, name="wt_codes", align_bytes=64)
        wt_bytes = keep.tile([P, R], U8, name="wt_bytes", align_bytes=64)

        nc.vector.tensor_copy(wt_bytes[:].rearrange("p (t m) -> p m t", t=PACK), wt_plane[:].indirect(list3[:]))

        def combine(pairs, u, left, right, op, lo, hi):
            nc.vector.tensor_tensor(
                pairs[:, u, lo:hi, :],
                left[u][:, :, lo:hi].rearrange("p e j -> p j e"),
                right[u][:, :, lo:hi].rearrange("p e j -> p j e"),
                op,
            )

        def weave(engine_copy, word, dst, pairs, lo, hi):
            words = pairs[:].rearrange("p u j e -> p u (j e)").bitcast(word)
            engine_copy(dst.bitcast(word).rearrange("p (j u) -> p j u", u=2), words[:, :, lo:hi].rearrange("p u j -> p j u"))

        xc_pairs = keep.tile([P, 2, J, 2], BF16, name="xc_pairs", tag="wt_plane_then_pairs", align_bytes=64)
        xc = [keep.tile([P, (hi - lo) * PACK], BF16, name="xc%d" % lo, align_bytes=64) for lo, hi in CHUNKS]

        combine(xc_pairs, 0, first, second, SUB, 0, J)
        nc.vector.tensor_copy(wt_codes[:].rearrange("p (t m) -> p m t", t=PACK), wt_store[:].indirect(list3[:]))

        banks = {}

        def quantise_multiply(c):
            lo, hi = CHUNKS[c]
            width = hi - lo
            codes = keep.tile([P, width], U32, name="xc_codes%d" % c, align_bytes=64)
            plane = keep.tile([P, width], U8, name="xc_plane%d" % c, align_bytes=64)
            nc.vector.quantize_mx(out=codes[:].bitcast(FP8X4), scales=plane[:], in_=xc[c][:])
            for t in range(PACK):
                banks[t, c] = psum.tile([P, width], F32, name="bank%d_%d" % (t, c), tag="bank%d_%d" % (t, c))
                nc.tensor.matmul_mx(
                    out=banks[t, c][:],
                    lhsT=wt_codes[:, t * P : (t + 1) * P].bitcast(FP8X4),
                    lhsT_scale=wt_bytes[:, t * P : (t + 1) * P],
                    rhs=codes[:].bitcast(FP8X4),
                    rhs_scale=plane[:],
                    start=True,
                    stop=True,
                )

        for lo, hi in PIECES:
            c = lo // 256
            combine(xc_pairs, 1, first, second, SUB, lo, hi)
            weave(nc.scalar.copy, U32, xc[c][:, PACK * (lo - 256 * c) : PACK * (hi - 256 * c)], xc_pairs, lo, hi)
        for c in range(len(CHUNKS)):
            quantise_multiply(c)

        def put_vector(t, lo, hi):
            c = lo // 256
            values = keep.tile([P, hi - lo], F32, name="values", tag="ring", bufs=2, align_bytes=64)
            nc.vector.tensor_copy(values[:], banks[t, c][:, lo - 256 * c : hi - 256 * c])
            nc.vector.tensor_copy(board[t][:].indirect(list4[:, lo // 16 : hi // 16]), values[:])

        def put_scalar(t, lo, hi):
            values = keep.tile([P, hi - lo], F32, name="values%d_%d" % (t, lo))
            for c, (c_lo, c_hi) in enumerate(CHUNKS):
                a, b = max(lo, c_lo), min(hi, c_hi)
                if a < b:
                    nc.scalar.copy(values[:, a - lo : b - lo], banks[t, c][:, a - c_lo : b - c_lo])
            nc.scalar.activation(board[t][:].indirect(list4[:, lo // 16 : hi // 16]), values[:], COPY)

        read_a = [keep.tile([P, 2, O], F32, name="read_a%d" % u) for u in range(2)]
        read_b = [keep.tile([P, 2, O], F32, name="read_b%d" % u) for u in range(2)]

        def fetch_a(t, lo, hi):
            nc.scalar.activation(
                read_a[t // 2][:, t % 2, lo:hi], board[t][:].indirect(list5[:, lo // 16 : hi // 16]), COPY, scale=weight_a[:, t : t + 1]
            )

        def fetch_b(t):
            nc.scalar.activation(read_b[t // 2][:, t % 2, :], board[t][:].indirect(list6[:]), COPY, scale=weight_b[:, t : t + 1])

        def fetch(t):
            fetch_a(t, 0, O)
            fetch_b(t)

        for lo, hi in CHUNKS:
            put_scalar(0, lo, hi)
            put_vector(1, lo, hi)
            put_vector(2, lo, hi)
        put_scalar(3, 0, SHARE3)
        put_vector(3, SHARE3, J)
        for t in range(PACK - 1):
            fetch(t)
        fetch_b(3)
        for lo, hi in HALVES:
            fetch_a(3, lo, hi)

        xr_codes = keep.tile([P, O], U32, name="xr_codes", tag="ring", bufs=2, align_bytes=64)
        xr_bytes = keep.tile([P, O], U8, name="xr_bytes", tag="ring", bufs=2, align_bytes=64)
        nc.vector.tensor_copy(xr_codes[:], xr_store[:].indirect(list7[:]))
        nc.vector.tensor_copy(xr_bytes[:], xr_plane[:].indirect(list7[:]))
        sums = {}
        for g, (lo, hi) in enumerate(HALVES):
            for h in range(2):
                sums[g, h] = psum.tile([P, UNIT], F32, name="sums%d_%d" % (g, h), tag="bank%d_%d" % (h + 1, g))
                nc.tensor.matmul_mx(
                    out=sums[g, h][:],
                    lhsT=ws_codes[:, h * P : (h + 1) * P].bitcast(FP8X4),
                    lhsT_scale=ws_plane[:, h * P : (h + 1) * P],
                    rhs=xr_codes[:, lo:hi].bitcast(FP8X4),
                    rhs_scale=xr_bytes[:, lo:hi],
                    start=True,
                    stop=False,
                )

        hid = [keep.tile([P, UNIT, PACK], BF16, name="hid%d" % lo, align_bytes=64) for lo, hi in HALVES]

        def larger(u, g):
            lo, hi = HALVES[g]
            nc.vector.tensor_tensor(
                hid[g][:, :, 2 * u : 2 * u + 2],
                read_a[u][:, :, lo:hi].rearrange("p e o -> p o e"),
                read_b[u][:, :, lo:hi].rearrange("p e o -> p o e"),
                MAX,
            )

        def finish(g, ways_out):
            lo, hi = HALVES[g]
            codes = keep.tile([P, UNIT], U32, name="hid_codes%d" % g, align_bytes=64)
            plane = keep.tile([P, UNIT], U8, name="hid_plane%d" % g, align_bytes=64)
            nc.vector.quantize_mx(out=codes[:].bitcast(FP8X4), scales=plane[:], in_=hid[g][:].rearrange("p o t -> p (o t)"))
            for h in range(2):
                nc.tensor.matmul_mx(
                    out=sums[g, h][:],
                    lhsT=wb_codes[:, 2 * h * P : 2 * (h + 1) * P].bitcast(FP4X4),
                    lhsT_scale=wb_plane[:, h * P : (h + 1) * P],
                    rhs=codes[:].bitcast(FP8X4),
                    rhs_scale=plane[:],
                    start=False,
                    stop=True,
                )
            for h, (engine_copy, queue) in enumerate(ways_out):
                result = keep.tile([P, UNIT], F32, name="result%d_%d" % (g, h))
                engine_copy(result[:], sums[g, h][:])
                queue.dma_start(out[h * P : (h + 1) * P, lo:hi], result[:])

        for u in range(2):
            for g in range(len(HALVES)):
                larger(u, g)
        finish(0, ((nc.scalar.copy, nc.sync), (nc.scalar.copy, nc.sync)))
        finish(1, ((nc.vector.tensor_copy, nc.sync), (nc.scalar.copy, nc.scalar)))
